import numpy as np, ml_dtypes
CORES = [2,3,42,43,82,83,122,123]
N = 8
BF = ml_dtypes.bfloat16
W, TU, RO, Q, S = 8192, 256, 4, 6, 32
HOPS = [1, 7]
BL = TU // len(HOPS)
def pack(x, l, w, k, h):
    return {"field": x.reshape(N, 128, W).astype(np.float32).astype(BF), "tube": np.ascontiguousarray(l.reshape(N, 128, TU)).astype(np.int32),
            "wt": w.reshape(N, 128, 1).astype(np.int32), "kn": k.reshape(N, 128, 1).astype(np.int32), "lim": np.ascontiguousarray(h.reshape(N, 128, RO)).astype(np.int32)}
def parts(rng):
    dark = rng.random((N, 8, 1, W)) < rng.choice(np.array([0.04, 0.08, 0.15]), (N, 8, 1, 1))
    x = np.where(dark, rng.integers(0, 64, (N, 8, 16, W), dtype=np.int16), rng.integers(48, 256, (N, 8, 16, W), dtype=np.int16))
    l = rng.integers(0, W, (N, 8, 16, TU)); w = rng.integers(0, 256, (N, 8, 16)); k = rng.integers(0, 256, (N, 8, 16))
    return x, l, w, k, rng.integers(16, 72, (N, 8, 16, RO))
def setup_inputs(rng):
    return pack(*parts(rng))
def setup_inputs_spread(rng):
    sh = rng.choice(np.array([0, 0, 0, 0, 0, 1, 1, 2, 4, 8], np.int16), (N, 8, 1, W))
    x = rng.integers(0, 256, (N, 8, 16, W), dtype=np.int16) >> sh
    l = rng.integers(0, W, (N, 8, 16, TU)); l[:, 1::2] = np.minimum((W * rng.random((N, 4, 16, TU)) ** 3).astype(np.int64), W - 1)
    w = rng.integers(0, 256, (N, 8, 16)) >> rng.integers(0, 9, (N, 8, 16)); k = rng.integers(0, 256, (N, 8, 16)) >> rng.integers(0, 9, (N, 8, 16))
    h = rng.integers(0, 249, (N, 8, 16, RO)) >> rng.integers(0, 9, (N, 8, 1, RO))
    return pack(x, l, w, k, h)
def ends_of(rng, hi, shape):
    return np.where(rng.random(shape) < 0.14, rng.integers(0, hi + 1, shape), hi * rng.integers(0, 2, shape))
def setup_inputs_ends(rng):
    kind = rng.random((N, 8, 1, W)); top = np.int16(255)
    x = np.where(kind < 0.7, top, np.where(kind < 0.82, np.int16(0), top * rng.integers(0, 2, (N, 8, 16, W), dtype=np.int16)))
    i = np.arange(16)[:, None]
    b = ((np.arange(N)[:, None] + np.arange(8)[None, :]) & 1) * (W - 1)
    l = np.where(i < rng.integers(0, 17, (N, 8, 1, TU)), b[:, :, None, None], (W - 1) * rng.integers(0, 2, (N, 8, 16, TU)))
    free = ((np.arange(TU) * 5) & 15) < 5; l[..., free] = rng.integers(0, W, (N, 8, 16, int(np.count_nonzero(free))))
    w = ends_of(rng, 255, (N, 8, 16)); k = ends_of(rng, 255, (N, 8, 16))
    h = 248 * rng.integers(0, 2, (N, 8, 16, RO)); h[:, 1::2] = 248 * rng.integers(0, 2, (N, 4, 1, RO))
    for q in range(N):
        for g in range(8):
            o = W - 1 - b[q, g]; x[q, g][:, b[q, g]] = 255
            x[q, g][:, o] = 0 if (g & 3) < 2 or q == 1 else 255 * rng.integers(0, 2, 16) if (g & 3) == 2 else 255
    h[0, :, :, 0] = 0; h[0, 0, :, 1] = 248; h[1, :, :, 0] = 248; h[1, 0, :, 1] = 0; l[1, :, 15, :] = (W - 1 - b[1])[:, None]
    h[2, :, :, 0] = 0; h[2, 0, :, 0] = 248; l[2, 0] = b[2, 0]; l[2, 0, 15, :7] = W - 1 - b[2, 0]; h[2, :, :, 1] = 248
    p = N - 1; u = (15 * 65025) & 4095
    for g in range(4, 8):
        x[p, g][:, 0] = 255; x[p, g][:, W - 1] = 255; w[p, g] = 255
        if g == 5: w[p, g] = 0; w[p, g, 0] = 16; w[p, g, 1] = 1; x[p, g, 1, 0] = 15; x[p, g, 1, W - 1] = 15
        if g > 5:
            w[p, g, 0] = 0; k[p, g] = 255 * (np.arange(16) & 1)
            for j in (0, W - 1):
                x[p, g][:, ((u * u >> 4) + j) & (W - 1)] = 0
                x[p, g][:, ((u * u >> 4) + 255 * u + j) & (W - 1)] = 255 if g == 6 else 0
    return pack(x, l, w, k, h)
def setup_inputs_corners(rng):
    x, l, w, k, h = parts(rng); i = np.arange(16)[:, None]; v = np.arange(TU)
    for q in range(N):
        for g in range(8):
            c = (g + q) & 7
            if c == 0: h[q, g] = 0
            if c == 1: h[q, g] = 248; x[q, g] = np.minimum(x[q, g], 247)
            if c == 2:
                s = rng.integers(0, W, TU); s[0] = 0; s[1] = W - 1; l[q, g] = s[None, :]
            if c == 3:
                m = np.where(rng.random(W) < 0.9, Q, Q - 1)[None, :]
                x[q, g] = np.where(i < m, rng.integers(150, 256, (16, W)), rng.integers(0, 90, (16, W))); h[q, g] = 100
            if c == 4: w[q, g] = 0; k[q, g] = 0
            if c == 5:
                m = rng.random(W) < 0.9; x[q, g, 0, m] = 255; x[q, g, 1, m] = 15; w[q, g] = 0; w[q, g, 0] = 16; w[q, g, 1] = 1; k[q, g] = 255 * rng.integers(0, 2, 16)
            if c == 6:
                t = rng.integers(0, 4, (16, TU)); l[q, g] = np.where(t == 0, 0, np.where(t == 1, W - 1, np.where(t == 2, S * v, S * v + S - 1)))
            if c == 7:
                x[q, g][:, 0::2] = rng.integers(200, 256, (16, W // 2)); x[q, g][:, 1::2] = rng.integers(0, 64, (16, W // 2)); h[q, g] = 100
                l[q, g] = 2 * rng.integers(0, W // 2, (16, TU)) + (i == (v % 17)[None, :])
    return pack(x, l, w, k, h)
def setup_inputs_ties(rng):
    x, l, w, k, h = parts(rng)
    pr = 60 + 4 * rng.integers(0, 3, (N, 8, 16, 5)); x = np.take_along_axis(pr, np.broadcast_to(rng.integers(0, 5, (N, 8, 1, W)), (N, 8, 16, W)), 3)
    return pack(x, l, w, k, rng.integers(53, 66, (N, 8, 16, RO)))
def setup_inputs_brink(rng):
    x, l, w, k, h = parts(rng); r0 = int(rng.integers(0, 8)); v = np.arange(TU)
    h[..., 0] = 0; h[..., 1] = 248; h[..., 2:] = rng.integers(246, 249, (N, 8, 1, RO - 2))
    for g in range(8):
        c = (g + r0) & 7; low = rng.permutation(W)[:32]
        for q in range(N):
            if c < 4:
                o = rng.permutation(16); y = np.full((16, W), 254); y[o[:Q]] = 255
                b = np.nonzero(rng.random(W) < 0.1)[0]; y[o[rng.integers(0, Q, len(b))], b] = 254
                x[q, g] = y
            elif c < 6:
                x[q, g] = rng.integers(248, 256, (16, W)); x[q, g][:, low] = rng.integers(7, 9, (16, 32))
            else:
                x[q, g] = rng.integers(243, 256, (16, W)); x[q, g][:, low] = rng.integers(0, 4, (16, 32))
            if c >= 4:
                l[q, g, rng.integers(1, 16, TU), v] = low[rng.integers(0, 32, TU)]; h[q, g] = 0
            if c == 0:
                d = int(rng.integers(0, W)); s = rng.integers(0, W - 1, (16, TU)); l[q, g] = s + (s >= d)
                l[q, g, rng.integers(1, 16, 7), rng.permutation(TU)[:7]] = d
                x[q, g][:, d] = rng.integers(0, 248, 16); h[q, g, :, 0] = 248
    return pack(x, l, w, k, h)
def check_inputs(d):
    bad = []
    for a, lo, hi in (("field", 0, 255), ("tube", 0, W - 1), ("wt", 0, 255), ("kn", 0, 255), ("lim", 0, 248)):
        v = np.asarray(d[a]).astype(np.float64)
        if not (np.min(v) >= lo and np.max(v) <= hi): bad.append("range of " + a)
        elif np.any(v != np.floor(v)): bad.append("whole numbers of " + a)
    return bad
def reference(field, tube, wt, kn, lim):
    x = field.astype(np.float32).astype(np.int32).reshape(N, 8, 16, W)
    l = tube.astype(np.int64).reshape(N, 8, 16, TU)
    w = wt.astype(np.int64).reshape(N, 8, 16, 1); k = kn.astype(np.int64).reshape(N, 8, 16, 1); h = lim.astype(np.int64).reshape(N, 8, 16, RO)
    cut = [0] * N; v = np.arange(TU); j = np.arange(16)[:, None]
    for rnd in range(RO):
        if rnd: l = np.concatenate([np.roll(l[..., b * BL:(b + 1) * BL], HOPS[b], axis=0) for b in range(len(HOPS))], axis=-1)
        nl = np.zeros((N, 8, 16, TU), np.int64); nz = np.zeros((N, 8, 16, TU), np.int64); ncut = [0] * N
        for q in range(N):
            for g in range(8):
                X, L = x[q, g], l[q, g]
                M = np.minimum.accumulate(X[:, L], axis=1)
                holds = (M >= (h[q, g, :, rnd] + (cut[q] & 7))[:, None, None]).astype(np.int64)
                ok = (np.add.reduce(holds, axis=0) >= Q).astype(np.int64)
                m = np.maximum(np.add.reduce(ok, axis=0), 1) - 1
                Z = np.take_along_axis(M, np.broadcast_to(m[None, None, :], (16, 1, TU)), 1)[:, 0].astype(np.int64)
                u = np.add.reduce(w[q, g] * X[:, L[m, v]], axis=0) & 4095
                c = ((u * u >> 4)[None, :] + k[q, g] * u[None, :] + L) & (W - 1)
                s = np.add.reduce(np.abs(X[:, c] - Z[:, None, :]), axis=0)
                best = c[np.argmin(s, axis=0), v]
                back = L[np.clip(m[None, :] + 1 - j, 0, 15), v[None, :]]
                nl[q, g] = np.where(j == 0, best[None, :], np.where(j <= m[None, :], back, c)); nz[q, g] = Z
                y = (Z + X[:, best]) >> 1
                x[q, g][:, S * v + (u & (S - 1))] = y
                ncut[q] += int(np.count_nonzero(m < 15))
        l = nl; cut = ncut
    return {"yl": l.reshape(N, 128, TU).astype(np.float32), "yz": nz.reshape(N, 128, TU).astype(np.float32)}

from concourse.mybir import AluOpType, AxisListType, ActivationFunctionType

A = AluOpType
F = ActivationFunctionType
RO = 4
BF, F32, I32, U16 = "bfloat16", "float32", "int32", "uint16"

SCRATCH = {}
for _b in "AB":
    for _n in ("p0", "p1", "p2", "p3"):
        SCRATCH[_n + _b] = ("psum", [128, 512], F32)
for _b in "AB":
    for _n in ("G", "M", "H", "Zx", "D", "AD"):
        SCRATCH[_n + _b] = ("sbuf", [128, 2048], BF)
    for _n, _d in (("Si", I32), ("Sm", I32), ("us", F32), ("Lp", F32), ("t32", I32), ("c32", I32), ("Wm", F32),
                   ("cm", F32), ("Rm", F32), ("OHc", F32), ("Km", F32), ("yh", I32), ("pass", BF),
                   ("OH", BF), ("Y", BF), ("zo", U16), ("cu", U16), ("ej", BF)):
        SCRATCH[_n + _b] = ("sbuf", [128, 128], _d)
    SCRATCH["pn" + _b] = ("sbuf", [128, 256], F32)
    SCRATCH["ys" + _b] = ("sbuf", [128, 256], F32)
    SCRATCH["ki" + _b] = ("sbuf", [128, 16], I32)
    SCRATCH["ku" + _b] = ("sbuf", [128, 8], U16)
    SCRATCH["su" + _b] = ("sbuf", [128, 384], U16)
    SCRATCH["sr" + _b] = ("sbuf", [128, 384], F32)
    for _t in range(RO):
        SCRATCH["win%d%s" % (_t, _b)] = ("sbuf", [128, 2048], F32)
        SCRATCH["lu%d%s" % (_t, _b)] = ("sbuf", [128, 128], U16)
for _n, _s, _d in (("X", [128, 8192], BF), ("R", [128, 1024], BF), ("Rk", [128, 128], F32), ("ones", [128, 256], BF),
                   ("E", [128, 144], BF), ("Bd", [128, 128], BF), ("Id", [128, 128], BF), ("Sh", [128, 128], BF),
                   ("selM", [128, 128], BF), ("Bn", [128, 128], BF), ("Wn", [128, 128], BF), ("Qe", [128, 128], BF),
                   ("R16", [128, 128], BF), ("mask", [128, 128], BF), ("K8", [128, 8], BF), ("wE", [128, 144], BF),
                   ("row16", [128, 128], BF), ("rowi", [128, 128], BF), ("Bd32", [128, 128], F32), ("Bu32", [128, 128], F32),
                   ("I32", [128, 128], F32), ("J32", [128, 128], F32), ("E32", [128, 144], F32), ("z8", [128, 16], F32),
                   ("cols", [128, 16], F32), ("wi", [128, 1], I32), ("kni", [128, 1], I32), ("limi", [128, 4], I32),
                   ("limf", [128, 4], F32), ("tub", [128, 256], I32), ("tubf", [128, 256], F32), ("pi", [128, 32], I32),
                   ("cvb", [128, 32], I32), ("cv", [128, 32], I32), ("zt", [128, 1920], F32), ("Wi", [128, 16], I32),
                   ("nu", [128, 32], I32), ("nv", [128, 32], I32), ("rp", [128, 32], U16), ("ei", [128, 2], I32),
                   ("ec", [128, 2], F32), ("one32", [128, 128], F32)):
    SCRATCH[_n] = ("sbuf", _s, _d)

SEMAPHORES = ["qV", "qA", "qT", "qG", "lX", "ltub", "lwt", "lkn", "llim", "snd", "out"]
for _b in "AB":
    SEMAPHORES += [_n + "%d%s" % (_t, _b) for _n in "wz" for _t in range(RO)]
    SEMAPHORES += ["au%d%s" % (_t, _b) for _t in range(1, RO)] + ["ar%d%s" % (_t, _b) for _t in range(1, RO)]

CY = 0.83e-3 * 1.2
PEC = 0.75e-3 * 1.2
GA = 1.5
WAKE = 0.12
PRI = dict(Abs0A=107,Abs0B=-224,Abs1A=-94,Abs1B=-31,Abs2A=-372,Abs2B=-627,Abs3A=322,Abs3B=-436,B=-69,CP0A=-224,CP0B=-356,
    CP1A=-370,CP1B=317,EA=254,EB=21,EaccA=523,EaccB=-161,G10A=387,G10B=-448,G11A=208,G11B=307,G20A=219,G20B=-180,G21A=-381,
    G21B=485,G22A=-937,G22B=216,G23A=41,G23B=40,KmA=913,KmB=-364,KpA=588,KpB=-12,LpA=-95,LpB=83,OHA=-510,OHB=54,OHTA=681,
    OHTB=168,OHcA=-216,OHcB=350,RmA=207,RmB=-136,S0A=523,S0B=90,S1A=679,S1B=279,SC0A=-114,SC0B=-22,SC1A=694,SC1B=-272,SqA=751,
    SqB=-6,WexpA=-632,WexpB=474,WmA=520,WmB=-166,WpA=203,WpB=248,YA=240,YB=39,ZcA=728,ZcB=-69,Zx0A=-97,Zx0B=129,Zx1A=-141,
    Zx1B=-374,Zx2A=-274,Zx2B=-130,Zx3A=-34,Zx3B=-221,cmA=3,cmB=334,cnt0A=125,cnt0B=-25,cnt1A=316,cnt1B=678,e1=-192,e2=11,
    e3=-250,k1A=-245,k1B=232,k2A=196,k2B=-74,k3A=125,k3B=377,kcA=-561,kcB=-194,keyA=126,keyB=649,nat1A=100,nat1B=230,nat2A=312,
    nat2B=509,npassA=-309,npassB=320,outA=413,outB=538,passA=566,passB=232,revA=113,revB=-114,revcA=-31,revcB=-222,s4A=382,
    s4B=582,s5A=187,s5B=567,s6A=-629,s6B=-145,s7A=103,s7B=640,s8A=345,s8B=-104,scanA=65,scanB=526,scatA=-30,scatB=-3,scrA=-60,
    scrB=-65,selA=866,selB=472,sendrA=70,sendrB=-10,senduA=211,senduB=505,suA=-195,suB=126,uA=823,uB=451,usA=-23,usB=-153,
    w1A=-76,w1B=20,w2=-71,w3=-305,w4=196,w5=557,yhA=-410,yhB=199,ylA=-41,ylB=-98,yzA=-366,yzB=306,zoA=518,zoB=141)
LOOK = {"V": 0.0, "A": 0.0, "T": 0.2, "G": 0.0, "S": 0.0, "AD": 0.0, "R": 0.0}
G1Q = {("A", 0): "A", ("A", 1): "V", ("B", 0): "A", ("B", 1): "A"}


def vcost(n, f=1.0): return 0.05 + max(64, n * f) * CY
def gcost(n): return 0.06 + n * GA * CY


def make_ops(core, T, topo):
    ops = []
    lastw, readers, bank = {}, {}, {}
    dcount = {}
    cur = [""]

    def op(q, cost, reads, writes, fn, banks=(), sem=None, cnt=0, sched=(), tag=""):
        o = {"i": len(ops), "q": q, "c": cost, "fn": fn, "wait": set(), "order": set(sched), "sem": sem, "tag": tag + cur[0], "n": cnt}
        for k in reads:
            if k in lastw: o["wait"].add(lastw[k])
        for k in writes:
            if k in lastw: o["wait"].add(lastw[k])
            for r in readers.get(k, ()):
                if ops[r]["q"] == q and q != "S": o["order"].add(r)
                else: o["wait"].add(r)
        for k in banks:
            if k in bank:
                r = bank[k]
                (o["order"] if ops[r]["q"] == q else o["wait"]).add(r)
            bank[k] = o["i"]
        for k in reads: readers.setdefault(k, []).append(o["i"])
        for k in writes:
            lastw[k] = o["i"]; readers[k] = []
        o["wait"].discard(o["i"]); o["order"].discard(o["i"])
        if q in ("S", "AD"):
            dcount[sem] = dcount.get(sem, 0) + 16
            o["n"] = dcount[sem]
        ops.append(o)
        return o["i"]

    def V(n, f, reads, writes, fn, banks=(), tag=""):
        return op("V", vcost(n, f), reads, writes, fn, banks, tag=tag)

    def C(n, reads, writes, fn, banks=(), tag=""):
        return op("A", 0.07 + max(64, n) * CY, reads, writes, fn, banks, tag=tag)

    def P(cyc, reads, fn, banks, tag=""):
        return op("T", 0.03 + cyc * PEC, reads, (), fn, banks, tag=tag)

    def Gc(n, reads, writes, fn, tag=""):
        return op("G", 0.17 + 2 * n * CY, reads, writes, fn, tag=tag)

    def DMA(q, cost, reads, writes, out, in_, sem, tag=""):
        return op(q, cost, reads, writes, lambda e: e.dma_start(out, in_), sem=sem, tag=tag)

    rank = T.rank_of(core)
    ncore = len(T.cores)
    peer = {"A": (T.cores[(rank + 1) % ncore], T.cores[(rank - 1) % ncore]),
            "B": (T.cores[(rank - 1) % ncore], T.cores[(rank + 1) % ncore])}

    def lanes(s, d):
        return topo.engines(s, d)[:8]

    DMA("AD", 2.0, (), ("tub",), T.tub[:], T.tube[:], "ltub")
    DMA("AD", 2.0, (), ("wi",), T.wi[:], T.wt[:], "lwt")
    DMA("AD", 2.0, (), ("kni",), T.kni[:], T.kn[:], "lkn")
    DMA("AD", 2.0, (), ("limi",), T.limi[:], T.lim[:], "llim")
    DMA("S", 11.0, (), ("X",), T.X[:], T.field[:], "lX")
    V(256, .5, (), ("ones",), lambda e: e.memset(T.ones[:], 1.0))
    V(128, 1, (), ("one32",), lambda e: e.memset(T.one32[:], 1.0))
    ON, O3 = T.ones, T.one32
    Gc(128, ("ones",), ("Bd0",), lambda e: e.affine_select(T.Bd[:], ON[:, 0:128], [[-16, 8], [0, 16]], A.is_ge, 0.0, 0, 1))
    Gc(128, ("Bd0",), ("Bd",), lambda e: e.affine_select(T.Bd[:], T.Bd[:], [[16, 8], [0, 16]], A.is_ge, 0.0, 15, -1))
    Gc(128, ("ones",), ("Id",), lambda e: e.affine_select(T.Id[:], ON[:, 0:128], [[-1, 128]], A.is_equal, 0.0, 0, 1))
    Gc(8, ("one32",), ("z8",), lambda e: e.affine_select(T.z8[:, 0:8], O3[:, 0:8], [[-16, 8]], A.is_equal, 0.0, 0, 1))
    Gc(128, ("one32",), ("J0",), lambda e: e.affine_select(T.J32[:], O3[:], [[-16, 8], [1, 16]], A.is_equal, 0.0, -16, 1))
    Gc(8, ("one32",), ("z15",), lambda e: e.affine_select(T.z8[:, 8:16], O3[:, 0:8], [[-16, 8]], A.is_equal, 0.0, -15, 1))
    Gc(144, ("ones",), ("E0",), lambda e: e.affine_select(T.E[:], ON[:, 0:144], [[0, 9], [1, 16]], A.is_equal, 0.0, -15, 0))
    Gc(144, ("E0",), ("E1",), lambda e: e.affine_select(T.E[:], T.E[:], [[-16, 9], [0, 16]], A.is_ge, 0.0, 0, 1))
    Gc(144, ("E1",), ("E",), lambda e: e.affine_select(T.E[:], T.E[:], [[16, 9], [0, 16]], A.is_ge, 0.0, 15, -1))
    Gc(128, ("ones",), ("Sh",), lambda e: e.affine_select(T.Sh[:], ON[:, 0:128], [[-1, 128]], A.is_equal, 0.0, -1, 1))
    Gc(128, ("ones",), ("R16",), lambda e: e.affine_select(T.R16[:], ON[:, 0:128], [[0, 8], [1, 16]], A.is_equal, 0.0, 0, -1))
    Gc(128, (), ("row16",), lambda e: e.iota(T.row16[:], [[16, 128]], 0, 0, allow_small_or_imprecise_dtypes=True))
    Gc(128, (), ("rowi",), lambda e: e.iota(T.rowi[:], [[0, 8], [1, 16]], 0, 0, allow_small_or_imprecise_dtypes=True))
    Gc(32, (), ("pi",), lambda e: e.iota(T.pi[:], [[0, 32]], 0, 1))
    Gc(16, (), ("cvb0",), lambda e: e.iota(T.cvb[:, 0:16], [[0, 2], [16, 8]], 0, 0))
    Gc(16, (), ("cvb1",), lambda e: e.iota(T.cvb[:, 16:32], [[512, 16]], 0, 0))
    for b in "AB":
        s = slice(0, 128) if b == "A" else slice(128, 256)
        V(128, 1, ("tub",), ("lu0" + b,), lambda e, b=b, s=s: e.tensor_copy(T["lu0" + b][:], T.tub[:, s]))
    V(256, 1, ("tub",), ("tubf",), lambda e: e.tensor_copy(T.tubf[:], T.tub[:]))
    for b in "AB":
        s = slice(0, 128) if b == "A" else slice(128, 256)
        P(512, ("J0", "tubf"), lambda e, b=b, s=s: e.matmul(T["p3" + b][:, 0:128], T.J32[:], T.tubf[:, s], True, True), ("3" + b,))
        C(128, (), ("win0%s.0" % b,), lambda e, b=b: e.activation(T["win0" + b][:, 0:128], T["p3" + b][:, 0:128], F.Copy), ("3" + b,))
    V(1920, 1, (), ("zt",), lambda e: e.memset(T.zt[:], 0.0))
    for t in range(RO):
        for b in "AB":
            DMA("S", 2.0, ("zt",), ("win%d%s.z" % (t, b),), T["win%d%s" % (t, b)][112:128, 128:2048], T.zt[112:128, :], "z%d%s" % (t, b))
    col = T.cols
    V(8, 1, ("z8",), ("c0",), lambda e: e.tensor_reduce(col[:, 0:1], T.z8[:, 0:8], AxisListType.X, A.add))
    V(8, 1, ("z15",), ("c2",), lambda e: e.tensor_reduce(col[:, 2:3], T.z8[:, 8:16], AxisListType.X, A.add, negate=True))
    V(1, 1, ("c0",), ("c1",), lambda e: e.tensor_scalar(col[:, 1:2], col[:, 0:1], -1.0, 1.0, A.mult, A.add))
    V(1, 1, ("c0",), ("c3",), lambda e: e.tensor_scalar(col[:, 3:4], col[:, 0:1], -7.0, 6.0, A.mult, A.add))
    V(1, 1, ("c0",), ("c8",), lambda e: e.tensor_scalar(col[:, 8:9], col[:, 0:1], 2048.0, -128.0, A.mult, A.add))
    V(1, 1, ("wi",), ("c4",), lambda e: e.tensor_copy(col[:, 4:5], T.wi[:]))
    V(1, 1, ("kni",), ("c5",), lambda e: e.tensor_scalar(col[:, 5:6], T.kni[:], 8.0, None, A.mult))
    V(1, 1, ("c5",), ("c9",), lambda e: e.tensor_tensor(col[:, 9:10], col[:, 5:6], col[:, 5:6], A.mult))
    V(1, 1, ("c9",), ("c6",), lambda e: e.tensor_scalar(col[:, 6:7], col[:, 9:10], -1.0, None, A.mult))
    V(4, 1, ("limi",), ("limf",), lambda e: e.tensor_copy(T.limf[:], T.limi[:]))
    V(144, .5, ("E", "c4"), ("wE",), lambda e: e.tensor_scalar(T.wE[:], T.E[:], col[:, 4:5], None, A.mult))
    V(1024, .5, (), ("R0",), lambda e: e.memset(T.R[:], 0.0))
    V(64, .5, ("R0",), ("R",), lambda e: e.memset(T.R[:, 0:1024:16], 255.0))
    V(128, 2, ("Sh", "Bd"), ("ShB",), lambda e: e.tensor_tensor(T.Sh[:], T.Sh[:], T.Bd[:], A.mult))
    V(128, 2, ("Id", "ShB"), ("selM",), lambda e: e.tensor_tensor(T.selM[:], T.Id[:], T.Sh[:], A.subtract))
    V(128, .5, ("Bd", "c1"), ("Bn",), lambda e: e.tensor_scalar(T.Bn[:], T.Bd[:], col[:, 1:2], None, A.mult))
    V(128, 1, ("Bd",), ("Bd32",), lambda e: e.tensor_copy(T.Bd32[:], T.Bd[:]))
    V(128, 1, ("Bd",), ("Bu32",), lambda e: e.tensor_scalar(T.Bu32[:], T.Bd[:], 2048.0, None, A.mult))
    V(128, .5, ("Bd", "c8"), ("Wn",), lambda e: e.tensor_scalar(T.Wn[:], T.Bd[:], col[:, 8:9], None, A.mult))
    V(128, .5, ("ones", "c2"), ("Qe",), lambda e: e.tensor_scalar(T.Qe[:], ON[:, 0:128], col[:, 2:3], None, A.mult))
    P(128, ("R16",), lambda e: e.matmul(T.p2A[:, 0:128], T.R16[:], T.R16[:], True, True), ("2A",))
    V(128, 1, (), ("mask",), lambda e: e.tensor_copy(T.mask[:], T.p2A[:, 0:128]), ("2A",))
    V(8, 1, ("Bd",), ("K8",), lambda e: e.tensor_scalar(T.K8[:], T.Bd[:, 0:128:16], 4096.0, None, A.mult))
    V(128, 1, ("Id", "c1"), ("I32",), lambda e: e.tensor_scalar(T.I32[:], T.Id[:], col[:, 1:2], None, A.mult))
    V(144, 1, ("E",), ("E32",), lambda e: e.tensor_copy(T.E32[:], T.E[:]))
    V(128, 1, (), ("Rk0",), lambda e: e.memset(T.Rk[:], 0.0))
    V(8, 1, ("Rk0",), ("Rk",), lambda e: e.memset(T.Rk[:, 0:128:16], 33554432.0))
    V(32, 1, ("pi",), ("pi2",), lambda e: e.tensor_scalar(T.pi[:], T.pi[:], 15, None, A.bitwise_and))
    V(16, 1, ("pi2",), ("pi3",), lambda e: e.tensor_scalar(T.pi[:, 16:32], T.pi[:, 16:32], 32, None, A.mult))
    V(32, 2, ("pi2", "pi3", "cvb0", "cvb1"), ("cv",), lambda e: e.tensor_tensor(T.cv[:], T.pi[:], T.cvb[:], A.add))
    V(1, 1, ("limf",), ("thr",), lambda e: e.tensor_copy(col[:, 7:8], T.limf[:, 0:1]))

    pend = {}
    for t in range(RO):
        last = t == RO - 1
        if t:
            for b in "AB":
                src = peer[b][1]
                op("R", 2.2, (), ("lu%d%s" % (t, b),), None, sem="au%d%s" % (t, b), cnt=len(lanes(src, core)), sched=(pend["u" + b],))
                op("R", 2.2, (), ("win%d%s.0" % (t, b),), None, sem="ar%d%s" % (t, b), cnt=len(lanes(src, core)), sched=(pend["r" + b],))
        for k in (1, 2, 4, 8):
            for b in "AB":
                w = T["win%d%s" % (t, b)]; n = "win%d%s." % (t, b)
                rd = [n + "z", n + "0"] + [n + str(j) for j in (1, 2, 4) if j < k]
                DMA("S", 2.0 + k * .06, rd, (n + str(k),), w[0:128 - k, 128 * k:256 * k], w[k:128, 0:128 * k], "w%d%s" % (t, b))
        for b in "AB":
            cur[0] = b
            bk = [str(j) + b for j in range(4)]
            p0, p1, p2, p3 = T["p0" + b], T["p1" + b], T["p2" + b], T["p3" + b]
            lu = T["lu%d%s" % (t, b)]; luk = "lu%d%s" % (t, b)
            tl = {n: T[n + b] for n in ("G", "M", "H", "Si", "Sm", "us", "Lp", "t32", "c32", "Wm", "pass", "zo", "cu", "ej", "Zx")}
            G, M, H, Zx = tl["G"], tl["M"], tl["H"], tl["Zx"]
            V(128, 1, (luk, "c6"), ("Lp" + b,), lambda e, d=tl["Lp"], s=lu: e.tensor_scalar(d[:], s[:], 16.0, col[:, 6:7], A.mult, A.add), tag="Lp")
            for h in (0, 1):
                f = slice(h * 1024, h * 1024 + 1024); o = slice(h * 64, h * 64 + 64)
                gk, mk, hk = "G%s%d" % (b, h), "M%s%d" % (b, h), "H%s%d" % (b, h)
                if G1Q[(b, h)] == "A":
                    op("A", gcost(1024), ("X", luk), (gk,), lambda e, G=G, f=f, o=o, lu=lu: e.activation(G[:, f], T.X[:, 0:8192].indirect(lu[:, o]), F.Copy), tag="G1%d" % h)
                else:
                    op("V", gcost(1024), ("X", luk), (gk,), lambda e, G=G, f=f, o=o, lu=lu: e.tensor_copy(G[:, f], T.X[:, 0:8192].indirect(lu[:, o])), tag="G1%d" % h)
                V(1024, .5, (gk, "R"), (mk,), lambda e, G=G, M=M, f=f: e.tensor_tensor_scan(M[:, f], T.R[:], G[:, f], 0.0, A.max, A.min), tag="SC%d" % h)
                V(1024, .5, (mk, "thr"), (hk,), lambda e, H=H, M=M, f=f: e.tensor_scalar(H[:, f], M[:, f], col[:, 7:8], None, A.is_ge), tag="CP%d" % h)

                def mm8(e, dst, w, src, i0, h=h, o=o):
                    for i in range(i0, i0 + 8):
                        r = e.matmul(dst[:, o], w[:, 15 - i:143 - i], src[:, h * 1024 + i:h * 1024 + 1024:16], i == 0, i == 15)
                    return r
                for i0 in (0, 8):
                    P(512, (gk, "wE"), lambda e, d=p1, s=G, f=mm8, i0=i0: f(e, d, T.wE, s, i0), (bk[1],), tag="S%d" % h)
                for i0 in (0, 8):
                    P(512, (hk, "E"), lambda e, d=p0, s=H, f=mm8, i0=i0: f(e, d, T.E, s, i0), (bk[0],), tag="cnt%d" % h)
            V(128, 1, (), ("Si" + b,), lambda e, d=tl["Si"], s=p1: e.tensor_copy(d[:], s[:, 0:128]), (bk[1],), tag="s7")
            V(128, 1, ("Si" + b,), ("Sm" + b,), lambda e, d=tl["Sm"], s=tl["Si"]: e.tensor_scalar(d[:], s[:], 4095, None, A.bitwise_and), tag="s8")
            V(128, 1, ("c3",), ("pass" + b,), lambda e, d=tl["pass"], s=p0: e.tensor_scalar(d[:], s[:, 0:128], col[:, 3:4], None, A.is_ge), (bk[0],), tag="pass")

            def selnoff(e, p2=p2, ps=tl["pass"]):
                e.matmul(p2[:, 0:128], T.selM[:], ps[:], True, True)
                e.matmul(p2[:, 128:256], ON[0:1, 0:128], T.row16[0:1, :], True, False)
                return e.matmul(p2[:, 128:256], T.Bn[:], ps[:], False, True)
            P(384, ("pass" + b, "selM", "Bn", "ones", "row16"), selnoff, (bk[2],), tag="sel")
            V(128, 1, ("Sm" + b,), ("us" + b,), lambda e, d=tl["us"], s=tl["Sm"], p2=p2: e.tensor_tensor(d[:], s[:], p2[:, 0:128], A.mult), (bk[2],), tag="us")
            V(128, 1, (), ("zo" + b,), lambda e, d=tl["zo"], p2=p2: e.tensor_copy(d[:], p2[:, 128:256]), (bk[2],), tag="zo")
            P(512, ("us" + b, "Bd32"), lambda e, d=p3, s=tl["us"]: e.matmul(d[:, 0:128], T.Bd32[:], s[:], True, True), (bk[3],), tag="u")
            C(128, ("c5",), (), lambda e, d=p3: e.activation(d[:, 128:256], d[:, 0:128], F.Square, bias=col[:, 5:6]), (bk[3],), tag="Sq")
            V(128, 1, ("Lp" + b,), ("t32" + b,), lambda e, d=tl["t32"], p3=p3, l=tl["Lp"]: e.tensor_tensor(d[:], p3[:, 128:256], l[:], A.add), (bk[3],), tag="s4")
            V(128, 1, ("t32" + b,), ("c32" + b,), lambda e, d=tl["c32"], s=tl["t32"]: e.tensor_scalar(d[:], s[:], 4, 8191, A.arith_shift_right, A.bitwise_and), tag="s5")
            V(128, 1, ("c32" + b,), ("cu" + b,), lambda e, d=tl["cu"], s=tl["c32"]: e.tensor_copy(d[:], s[:]), tag="s6")
            for h4 in range(4):
                f = slice(h4 * 512, h4 * 512 + 512); o = slice(h4 * 32, h4 * 32 + 32)
                op("A", gcost(512), ("zo" + b, "M%s0" % b, "M%s1" % b), ("Zx%s%d" % (b, h4),),
                   lambda e, d=Zx, M=M, z=tl["zo"], f=f, o=o: e.activation(d[:, f], M[:, 0:2048].indirect(z[:, o]), F.Copy), tag="Zx%d" % h4)
            C(128, ("pass" + b,), (), lambda e, d=p3, s=tl["pass"]: e.activation(d[:, 256:384], s[:], F.Copy, bias=1.0, scale=-1.0), (bk[3],), tag="npass")

            def wexp(e, p1=p1, ps=tl["pass"], us=tl["us"], last=last):
                r = e.matmul(p1[:, 128:256], ps[:], T.Wn[:], True, last)
                if not last:
                    r = e.matmul(p1[:, 128:256], us[:], T.Bu32[:], False, True)
                return r
            P(640, ("pass" + b, "us" + b, "Wn", "Bu32"), wexp, (bk[1],), tag="Wexp")
            V(128, 1, ("mask",), ("Wm" + b,), lambda e, d=tl["Wm"], p1=p1: e.tensor_tensor(d[:], p1[:, 128:256], T.mask[:], A.mult), (bk[1],), tag="Wm")
            P(256, ("Wm" + b, "Bd32"), lambda e, p1=p1, s=tl["Wm"]: e.matmul(p1[:, 256:264], s[:], T.Bd32[:, 0:128:16], True, True), (bk[1],), tag="Wp")
            c0 = 0 if b == "A" else 8
            V(8, 1, (), ("Wi" + b,), lambda e, p1=p1, c0=c0: e.tensor_copy(T.Wi[:, c0:c0 + 8], p1[:, 256:264]), (bk[1],), tag="w1")
            if not last:
                P(128, ("Qe", "pass" + b), lambda e, d=p0, s=tl["pass"]: e.matmul(d[:, 128:256], T.Qe[:], s[:], True, True), (bk[0],), tag="E")
                ec = T.ec[:, 0:1] if b == "A" else T.ec[:, 1:2]
                C(128, (), ("ec" + b, "ej" + b), lambda e, d=tl["ej"], s=p0, c=ec: e.activation(d[:], s[:, 128:256], F.Copy, accum_out=c), (bk[0],), tag="Eacc")
        cur[0] = ""
        V(16, 1, ("WiA", "WiB"), ("nu0",), lambda e: e.tensor_scalar(T.nu[:, 0:16], T.Wi[:], 2047, None, A.bitwise_and), tag="w2")
        if last:
            V(16, 2, ("nu0", "cv"), ("nv",), lambda e: e.tensor_tensor(T.nv[:, 0:16], T.nu[:, 0:16], T.cv[:, 0:16], A.add), tag="w4")
            V(16, 1, ("nv",), ("rp",), lambda e: e.tensor_copy(T.rp[:, 0:16], T.nv[:, 0:16]), tag="w5")
        else:
            V(16, 1, ("WiA", "WiB"), ("nu1",), lambda e: e.tensor_scalar(T.nu[:, 16:32], T.Wi[:], 11, 31, A.arith_shift_right, A.bitwise_and), tag="w3")
            V(32, 2, ("nu0", "nu1", "cv"), ("nv",), lambda e: e.tensor_tensor(T.nv[:], T.nu[:], T.cv[:], A.add), tag="w4")
            V(32, 1, ("nv",), ("rp",), lambda e: e.tensor_copy(T.rp[:], T.nv[:]), tag="w5")
            V(1, 1, ("ecA", "ecB"), ("ei",), lambda e: e.tensor_tensor(T.ei[:, 0:1], T.ec[:, 0:1], T.ec[:, 1:2], A.add), tag="e1")
            V(1, 1, ("ei",), ("ej2",), lambda e: e.tensor_scalar(T.ei[:, 1:2], T.ei[:, 0:1], 7, None, A.bitwise_and), tag="e2")
            V(1, 2, ("ej2", "limf"), ("thr",), lambda e, t=t: e.tensor_tensor(col[:, 7:8], T.ei[:, 1:2], T.limf[:, t + 1:t + 2], A.add), tag="e3")
        for b in "AB":
            cur[0] = b
            D, AD, Zx, cu = T["D" + b], T["AD" + b], T["Zx" + b], T["cu" + b]
            for h in range(4):
                f = slice(h * 512, h * 512 + 512); o = slice(h * 32, h * 32 + 32)
                op("V", gcost(512), ("X", "cu" + b, "Zx%s%d" % (b, h)), ("D%s%d" % (b, h),),
                   lambda e, D=D, Zx=Zx, cu=cu, f=f, o=o: e.tensor_tensor(D[:, f], T.X[:, 0:8192].indirect(cu[:, o]), Zx[:, f], A.subtract), tag="G2%d" % h)
                C(512, ("D%s%d" % (b, h),), ("AD%s%d" % (b, h),), lambda e, D=D, AD=AD, f=f: e.activation(AD[:, f], D[:, f], F.Abs), tag="Abs%d" % h)
        for b in "AB":
            cur[0] = b
            bk = [str(j) + b for j in range(4)]
            p0, p1, p2, p3 = T["p0" + b], T["p1" + b], T["p2" + b], T["p3" + b]
            D, AD, Zx, pn = T["D" + b], T["AD" + b], T["Zx" + b], T["pn" + b]
            q4 = [b + str(j) for j in range(4)]
            zk = ["Zx" + j for j in q4]
            q = {n: T[n + b] for n in ("cm", "Rm", "OHc", "Km", "yh", "pass", "OH", "Y", "c32", "ki", "ku")}
            c0 = 0 if b == "A" else 8
            V(128, 1, ("c32" + b,), ("cm" + b,), lambda e, q=q, p3=p3: e.tensor_tensor(q["cm"][:], q["c32"][:], p3[:, 256:384], A.mult), (bk[3],), tag="cm")
            if not last:
                C(128, zk, (), lambda e, d=p3, Zx=Zx: e.activation(d[:, 384:512], Zx[:, 0:2048:16], F.Copy), (bk[3],), tag="Zc")
            wn = "win%d%s" % (t, b)
            op("V", gcost(128), [wn + "." + j for j in "z01248"] + ["rp", "pass" + b], ("Rm" + b,),
               lambda e, q=q, w=T[wn], c0=c0: e.tensor_tensor(q["Rm"][:], w[:, 0:2048].indirect(T.rp[:, c0:c0 + 8]), q["pass"][:], A.mult), tag="Rm")
            if not last:
                def rev(e, p3=p3, q=q):
                    e.matmul(p3[:, 0:128], T.J32[:], q["cm"][:], True, False)
                    return e.matmul(p3[:, 0:128], T.J32[:], q["Rm"][:], False, True)
                P(1024, ("J0", "cm" + b, "Rm" + b), rev, (bk[3],), tag="rev")
                ts = slice(t * 128, t * 128 + 128)
                sr = T["sr" + b][:, ts]; su = T["su" + b][:, ts]
                C(128, (), ("sr%d%s" % (t, b),), lambda e, d=sr, p3=p3: e.activation(d, p3[:, 0:128], F.Copy), (bk[3],), tag="revc")
                pend["r" + b] = op("G", 1.0, ("sr%d%s" % (t, b),), (), ("send", sr, "win%d%s" % (t + 1, b), "ar%d%s" % (t + 1, b), peer[b][0]), sem="snd", tag="sendr")

            def nat1(e, p2=p2, q=q):
                e.matmul(p2[:, 0:128], T.I32[:], q["cm"][:], True, False)
                return e.matmul(p2[:, 0:128], T.I32[:], q["Rm"][:], False, False)
            P(1024, ("I32", "cm" + b, "Rm" + b), nat1, (bk[2],), tag="nat1")

            def kc(e, p0=p0):
                e.matmul(p0[:, 256:384], T.row16[0:1, :], ON[0:1, 0:128], True, False)
                return e.matmul(p0[:, 256:384], ON[0:1, 0:128], T.rowi[0:1, :], False, False)
            P(256, ("row16", "ones", "rowi"), kc, (bk[0],), tag="kc")

            def kd(e, p0=p0, AD=AD):
                for i in range(16):
                    r = e.matmul(p0[:, 256 + i:384:16], AD[:, i:2048:16], T.K8[:], False, i == 15)
                return r
            P(1024, ["AD" + j for j in q4] + ["K8"], kd, (bk[0],), tag="key")
            V(128, 1, ("Rk",), ("pm" + b,), lambda e, d=pn, p0=p0: e.tensor_tensor_scan(d[:, 0:128], T.Rk[:], p0[:, 256:384], 0.0, A.max, A.min), (bk[0],), tag="scan")
            V(128, 1, ("Rk", "pm" + b), ("mn" + b,), lambda e, d=pn: e.tensor_tensor_scan(d[:, 255:127:-1], T.Rk[:], d[:, 127::-1], 0.0, A.max, A.min), tag="scr")
            if not last:
                V(128, 2, ("mn" + b, "mask"), ("Km" + b,), lambda e, q=q, d=pn: e.tensor_tensor(q["Km"][:], d[:, 128:256], T.mask[:], A.mult), tag="Km")
            V(128, 1, ("mn" + b,), ("OH" + b,), lambda e, q=q, d=pn, p0=p0: e.tensor_tensor(q["OH"][:], p0[:, 256:384], d[:, 128:256], A.is_equal), (bk[0],), tag="OH")
            if not last:
                P(256, ("Km" + b, "Bd32"), lambda e, q=q, p0=p0: e.matmul(p0[:, 384:392], q["Km"][:], T.Bd32[:, 0:128:16], True, True), (bk[0],), tag="Kp")
            P(128, ("OH" + b, "Id"), lambda e, q=q, p1=p1: e.matmul(p1[:, 0:128], q["OH"][:], T.Id[:], True, True), (bk[1],), tag="OHT")
            V(128, 1, ("c32" + b,), ("OHc" + b,), lambda e, q=q, p1=p1: e.tensor_tensor(q["OHc"][:], q["c32"][:], p1[:, 0:128], A.mult), (bk[1],), tag="OHc")
            P(512, ("E32", "OHc" + b), lambda e, q=q, p2=p2: e.matmul(p2[:, 0:128], T.E32[:, 15:143], q["OHc"][:], False, True), (bk[2],), tag="nat2")
            if last:
                s = slice(0, 128) if b == "A" else slice(128, 256)
                ys = T["ys" + b]
                V(128, 1, (), ("yls" + b,), lambda e, d=ys, p2=p2: e.tensor_copy(d[:, 0:128], p2[:, 0:128]), (bk[2],), tag="yl")
                C(128, zk, ("yzs" + b,), lambda e, d=ys, Zx=Zx: e.activation(d[:, 128:256], Zx[:, 0:2048:16], F.Copy), tag="yz")
                DMA("S", 2.0, ("yzs" + b,), (), T.yz[:, s], ys[:, 128:256], "out", tag="out")
                DMA("S", 2.0, ("yls" + b,), (), T.yl[:, s], ys[:, 0:128], "out", tag="out")
            else:
                V(128, 1, (), ("su%d%s" % (t, b),), lambda e, d=su, p2=p2: e.tensor_copy(d, p2[:, 0:128]), (bk[2],), tag="su")
                pend["u" + b] = op("G", 1.0, ("su%d%s" % (t, b),), (), ("send", su, "lu%d%s" % (t + 1, b), "au%d%s" % (t + 1, b), peer[b][0]), sem="snd", tag="sendu")
                V(8, 1, (), ("ki" + b,), lambda e, q=q, p0=p0: e.tensor_copy(q["ki"][:, 0:8], p0[:, 384:392]), (bk[0],), tag="k1")
                V(8, 1, ("ki" + b,), ("kj" + b,), lambda e, q=q: e.tensor_scalar(q["ki"][:, 8:16], q["ki"][:, 0:8], 4095, None, A.bitwise_and), tag="k2")
                V(8, 1, ("kj" + b,), ("ku" + b,), lambda e, q=q: e.tensor_copy(q["ku"][:], q["ki"][:, 8:16]), tag="k3")
                op("V", gcost(128), ["ku" + b] + ["D" + j for j in q4], ("yh" + b,),
                   lambda e, q=q, D=D: e.tensor_scalar(q["yh"][:], D[:, 0:2048].indirect(q["ku"][:]), 0.5, -0.25, A.mult, A.add), tag="yh")
                V(128, 1, ("yh" + b,), ("Y" + b,), lambda e, q=q, p3=p3: e.tensor_tensor(q["Y"][:], q["yh"][:], p3[:, 384:512], A.add), (bk[3],), tag="Y")
                op("V", 0.06 + 128 * 3.5 * CY, ("Y" + b, "rp"), ("X",),
                   lambda e, q=q, c0=c0: e.tensor_copy(T.X[:, 0:8192].indirect(T.rp[:, 16 + c0:24 + c0]), q["Y"][:]), tag="scat")
    return ops, lanes, peer


def schedule(ops):
    n = len(ops)
    succ = [[] for _ in range(n)]
    for o in ops:
        for d in o["wait"] | o["order"]: succ[d].append(o["i"])
    pr = [0.0] * n
    for i in range(n - 1, -1, -1):
        pr[i] = ops[i]["c"] + max([pr[s] + (WAKE if ops[s]["q"] != ops[i]["q"] else .02) for s in succ[i]], default=0.0)
    need = [len(o["wait"] | o["order"]) for o in ops]
    ready, fin, avail, order = {}, [0.0] * n, {}, []
    rt = [0.0] * n
    for i in range(n):
        if not need[i]: ready[i] = 0.0
    while ready:
        st = {}
        for i, r in ready.items():
            q = ops[i]["q"]; q = "A" if q == "AD" else q
            st[i] = max(r, avail.get(q, 0.0)) if q != "R" else r
        best = {}
        for i in st:
            q = ops[i]["q"]
            if q not in best or st[i] < best[q]: best[q] = st[i]
        q0 = min(best, key=lambda q: best[q])
        cand = [i for i in st if ops[i]["q"] == q0 and st[i] <= best[q0] + LOOK[q0]]
        i = max(cand, key=lambda k: (pr[k] + PRI.get(ops[k]["tag"], 0.0), -k))
        o = ops[i]; q = "A" if o["q"] == "AD" else o["q"]
        s = st[i]
        fin[i] = s + o["c"]
        if q != "R": avail[q] = s + (0.1 if o["q"] in ("AD", "S") else o["c"])
        o["s"] = s
        order.append(i)
        del ready[i]
        for k in succ[i]:
            need[k] -= 1
            wk = WAKE if ops[k]["q"] != o["q"] else .05
            rt[k] = max(rt[k], fin[i] + wk)
            if not need[k]: ready[k] = rt[k]
    return order, max(fin)


def rank_program(g, core, T, topo):
    if T.rank_of(core) is None:
        return
    ops, lanes, peer = make_ops(core, T, topo)
    order, est = schedule(ops)
    eng = {"V": g.vector, "A": g.scalar, "T": g.tensor, "G": g, "S": g.sync, "AD": g.scalar}
    qsem = {"V": "qV", "A": "qA", "T": "qT", "G": "qG"}
    cnt, known, snap, done = {}, {}, {}, {}
    sent = 0
    for i in order:
        o = ops[i]
        if o["q"] == "R":
            done[i] = (o["sem"], o["n"]); snap[i] = {o["sem"]: o["n"]}
            continue
        qn = "A" if o["q"] == "AD" else o["q"]
        e = eng[o["q"]]
        kn = known.setdefault(qn, {})
        for d in sorted(o["wait"], key=lambda d: -ops[d].get("s", 0.0)):
            s, v = done[d]
            if kn.get(s, 0) >= v: continue
            e.wait_ge(T.sem[s], v)
            for k, x in snap[d].items():
                if kn.get(k, 0) < x: kn[k] = x
        if o["sem"] == "snd":
            _, src, dst, sem, to = o["fn"]
            ln = lanes(core, to)
            rid, pid, _ = topo.addr(to)
            g.remote_dma(out_ap=T[dst][:, 0:128], in_ap=src, remote_sem=T.sem[sem], local_sem=T.sem.snd, pid=pid, routing_id=rid,
                         dma_engine_mask=sum(1 << x for x in ln))
            sent += len(ln)
            done[i] = ("snd", sent); snap[i] = dict(kn)
        else:
            r = o["fn"](e)
            if o["q"] in ("S", "AD"):
                r.then_inc(T.sem[o["sem"]], 16)
                done[i] = (o["sem"], o["n"]); cnt[o["sem"]] = o["n"]
            else:
                s = qsem[o["q"]]
                cnt[s] = cnt.get(s, 0) + 1
                r.then_inc(T.sem[s], 1)
                done[i] = (s, cnt[s])
            snap[i] = dict(kn); snap[i][done[i][0]] = done[i][1]
    for s, v in cnt.items():
        g.wait_ge(T.sem[s], v)
    g.wait_ge(T.sem.snd, sent)
    for o in ops:
        if o["q"] == "R": g.wait_ge(T.sem[o["sem"]], o["n"])
